import numpy as np, ml_dtypes
CORES = [5,29,101,125,133,157,229,253]
N = 8
import mx_ref
BF = ml_dtypes.bfloat16
def entries(a):
    return np.ascontiguousarray(a.T).reshape(-1)
def table(e):
    return np.ascontiguousarray(np.reshape(e, (-1, 16)).T).astype(np.int32)
def cols(t, e):
    v = np.concatenate([t.reshape(128, -1, 4), np.zeros((128, 1, 4), BF)], axis=1)
    return np.ascontiguousarray(v[:, e]).reshape(128, -1)
def cut(t, i, w=512):
    return t[:, w * i:w * i + w]
def f(rng, *shape):
    return mx_ref.flush((rng.standard_normal(shape, dtype=np.float32) * np.exp2(rng.integers(-2, 3, shape[:-1] + (1,)))).astype(BF))
def wide(rng, *shape, cols=0):
    v = rng.standard_normal(shape, dtype=np.float32) * np.exp2(rng.integers(-12, 13, shape)).astype(np.float32)
    if cols: v *= np.repeat(np.exp2(rng.integers(-cols, cols + 1, shape[:-2] + (1, shape[-1] // 4))) * (rng.random(shape[:-2] + (1, shape[-1] // 4)) > 0.0625), 4, axis=-1).astype(np.float32)
    return mx_ref.flush(v.astype(BF))
TB, T, CAPP, O = 256, 256, 32, 1
def lists(rng, case=""):
    o = []; odd = rng.permutation(N)
    for r in range(N):
        lo, hi = {"one": (1, 1), "full": (CAPP, CAPP), "runs": (1, CAPP // 2), "none": (1, CAPP)}.get(case, (0, CAPP))
        n = rng.integers(lo, hi + 1, N)
        if case == "none":
            if r == odd[0]: n[:] = 0; n[rng.integers(0, N)] = 1
            elif r == odd[1]: n[r] = 0
            elif r == odd[2]: n[np.arange(N) != r] = 0
            else: n[rng.permutation(N)[:rng.integers(1, N)]] = 0
        if n.sum() == 0: n[rng.integers(0, N)] = 1
        if case == "full": named = [np.append([0, TB - 1], 1 + rng.permutation(TB - 2)[:n[q] - 2]) for q in range(N)]
        else: named = [rng.permutation(TB)[:n[q]] for q in range(N)]
        pool = rng.permutation(np.concatenate([q * TB + named[q] for q in range(N)]))
        i = np.arange(len(pool))
        k = T - len(pool)
        i = np.concatenate([i, (rng.random(k) * rng.random(k) * len(pool)).astype(int)])
        i = np.sort(i) if case == "runs" else rng.permutation(i)
        o.append(table(pool[i]))
    return {"want": np.stack(o)}
def setup_inputs(rng):
    return {"x": f(rng, N, 128, 4 * TB), "w": f(rng, N, 128, 512 * O), **lists(rng)}
def setup_inputs_one(rng):
    return {**setup_inputs(rng), **lists(rng, "one")}
def setup_inputs_full(rng):
    return {**setup_inputs(rng), **lists(rng, "full")}
def setup_inputs_runs(rng):
    return {**setup_inputs(rng), **lists(rng, "runs")}
def setup_inputs_none(rng):
    return {**setup_inputs(rng), **lists(rng, "none")}
def setup_inputs_spread(rng):
    d = setup_inputs(rng); d["x"] = wide(rng, N, 128, 4 * TB, cols=8); return d
def check_inputs(d):
    b = []
    for r in range(N):
        e = entries(d["want"][r])
        if e.min() < 0 or e.max() >= N * TB or any(len(np.unique(e[e // TB == q])) > CAPP for q in range(N)): b.append("want")
    return b
def reference(x, w, want):
    every = np.concatenate([x[q] for q in range(N)], axis=1)
    y = np.zeros((N, 128, O * T), np.float32)
    for r in range(N):
        t = mx_ref.quantize(cols(every, entries(want[r])))
        for o in range(O):
            y[r][:, T * o:T * o + T] = mx_ref.matmul(mx_ref.quantize(np.ascontiguousarray(cut(w[r], o))), t)
    return {"y": y}

@@ -1,0 +1,296 @@
+from concourse.bass import DstId, RemoteDMATransfer
+from concourse.mybir import dt, AluOpType, ActivationFunctionType
+
+OP = AluOpType
+COPY = ActivationFunctionType.Copy
+XW = 272
+PW = 2432
+
+SCRATCH = {"wt": ("sbuf", [64, 16], "int32"), "m0": ("psum", [128, 512], "float32"), "m1": ("psum", [128, 512], "float32")}
+for _t, _b in (("int32", "pi 1 pm 1 odd 1"),
+               ("uint16", "w16 16 w2 32 jj 4 msg 4 la 12 lb 16 oa 8 ob 8 rl 4 ou 16 oy 16"),
+               ("float32", "z2 2 s0 1 gsc 1 ua 16 fu 16 u1 16 u2 16 u3 16 nb 16 dd 16 ys 256 yo 256"),
+               ("bfloat16", "vwin %d cwin 2048 ones 256 cst 256 row 256 crow 272 rt 256 ne 1152 sc 1152 fr 256 qf 256 "
+                            "ge 256 gh 256 cc 256 le 512 nn 512 lg 64 lt 64 xt %d xs %d wb 512 ta 512 tb 512 vp 256 "
+                            "pr 512 pt 512" % (PW, 4 * XW, 4 * XW)),
+               ("float8_e4m3fn_x4", "qw 128 qa 128 qb 128 ca 128 cb 128 rc 64"),
+               ("uint8", "pw 128 pa 128 pb 128 da 128 db 128 rs 64")):
+    _w = _b.split()
+    for _i in range(0, len(_w), 2):
+        SCRATCH[_w[_i]] = ("sbuf", [128, int(_w[_i + 1])], _t)
+SEMAPHORES = "ld ldx ldw v s ps te aa ab ac ad own st su loc rl rc rs".split()
+
+
+def plane_of(topo, cores, r):
+    return [k for k in range(len(cores)) if k == r or topo.same_plane(cores[k], cores[r])]
+
+
+def roads(topo, cores, r):
+    mine = plane_of(topo, cores, r)
+    far = [k for k in range(len(cores)) if k not in mine]
+    c = cores[r]
+    able = [k for k in topo.cores_of(c) if k != c and all(topo.may_write(k, cores[f]) for f in far)]
+    pair = [[k for k in able if topo.die(k) == topo.die(c)][0], [k for k in able if topo.die(k) != topo.die(c)][0]]
+    a = mine.index(r)
+    return [(pair[h], [f for b, f in enumerate(far) if (a + b) % 2 == h]) for h in range(2)]
+
+
+def xfer(topo, src_core, dst_core, engines, sem, src, dst):
+    rid, pid = topo.addr(dst_core, src_core)
+    return RemoteDMATransfer(dst_ids=[DstId(rid=rid, pnc=pid)], dma_engine_mask=sum(1 << k for k in engines),
+                             remote_sem=sem, srcs=[src], dsts=[dst], alu_op=0)
+
+
+def u8(view):
+    return view.bitcast(dt.uint8)
+
+
+def relay(g, core, T, topo, r, ranks):
+    cores = T.cores
+    me = plane_of(topo, cores, r).index(r)
+    en = topo.engines(core, cores[ranks[0]])
+    half = [en[0:len(en) // 2], en[len(en) // 2:]]
+
+    def place(f):
+        return [k for _, ks in roads(topo, cores, f) for k in ks].index(r)
+    g.wait_ge(T.sem.rl, 4)
+    g.remote_dma_fused([xfer(topo, core, cores[f], half[i], T.sem.ab, T.rl[:, 0:4], T.lb[:, 4 * place(f):4 * place(f) + 4])
+                        for i, f in enumerate(ranks)], local_sem=T.sem.loc)
+    g.wait_ge(T.sem.rc, 4)
+    g.remote_dma_fused([xfer(topo, core, cores[f], half[i], T.sem.ad, u8(T.rc[:, 32 * i:32 * i + 32]),
+                             u8(T.cb[:, 32 * me:32 * me + 32])) for i, f in enumerate(ranks)], local_sem=T.sem.loc)
+    g.wait_ge(T.sem.rs, 4)
+    g.remote_dma_fused([xfer(topo, core, cores[f], half[i], T.sem.ad, T.rs[:, 32 * i:32 * i + 32],
+                             T.db[:, 32 * me:32 * me + 32]) for i, f in enumerate(ranks)], local_sem=T.sem.loc)
+    g.wait_ge(T.sem.loc, 3 * len(en))
+
+
+def rank_program(g, core, T, topo):
+    cores = T.cores
+    r = T.rank_of(core)
+    if r is None:
+        for k in range(len(cores)):
+            if core in topo.cores_of(cores[k]):
+                for c, ranks in roads(topo, cores, k):
+                    if c == core:
+                        relay(g, core, T, topo, k, ranks)
+        return
+    S = T.sem
+    plane = plane_of(topo, cores, r)
+    others = [k for k in plane if k != r]
+    road = roads(topo, cores, r)
+    far = [k for k in range(len(cores)) if k not in plane]
+    me = plane.index(r)
+    V, A, D, P = g.vector, g.scalar, g.sync, g.tensor
+    n = {"v": 0, "s": 0, "ps": 0}
+
+    def count(name, call):
+        call.then_inc(S[name], 1)
+        n[name] += 1
+        return n[name]
+
+    def v(call):
+        return count("v", call)
+
+    def s(call):
+        return count("s", call)
+
+    def ps(call):
+        return count("ps", call)
+
+    def vw():
+        V.wait_ge(S.v, n["v"])
+
+    D.dma_start(T.wt[0:16, :], T.want[:, :]).then_inc(S.ld, 16)
+    A.dma_start(T.wt[16:32, :], T.want[:, :]).then_inc(S.ld, 16)
+    D.dma_start(T.wt[32:48, :], T.want[:, :]).then_inc(S.ld, 16)
+    A.dma_start(T.wt[48:64, :], T.want[:, :]).then_inc(S.ld, 16)
+    D.dma_start(T.xt[:, 0:1024], T.x[:, :]).then_inc(S.ldx, 16)
+    D.dma_start(T.wb[:, :], T.w[:, :]).then_inc(S.ldw, 16)
+
+    small = {"allow_small_or_imprecise_dtypes": True}
+    g_v = ps(g.iota(T.vwin[:, 0:128], [[1, 128]], 128, 0, **small))
+    g_c = ps(g.iota(T.cwin[:, 0:256], [[1, 256]], 0, 0, **small))
+    g_p = ps(g.iota(T.pi[:, 0:1], [[0, 1]], 0, 1))
+    for a in range(4):
+        g.wait_ge(S.ps, n["ps"])
+        g_k = ps(g.iota(T.cst[32 * a:32 * a + 32, 0:256], [[-32, 8], [0, 32]], 256, -1, **small))
+    g.wait_ge(S.ps, g_k)
+
+    v(V.memset(T.ones[:, :], 1.0))
+    v(V.memset(T.crow[:, 256:272], 256.0))
+    v(V.memset(T.xt[:, 1024:4 * XW], 0.0))
+    v(V.memset(T.z2[:, :], 0.0))
+    V.wait_ge(S.ps, g_v)
+    for k, f in ((128, 2.0), (256, 4.0), (512, 16.0), (1024, 256.0)):
+        v_k = v(V.tensor_scalar(T.vwin[:, k:2 * k], T.vwin[:, 0:k], f, None, OP.mult))
+        vw()
+    V.wait_ge(S.ps, g_p)
+    v(V.tensor_scalar(T.odd[:, :], T.pi[:, :], 4, 1, OP.arith_shift_right, OP.bitwise_and))
+    v(V.tensor_scalar(T.pm[:, :], T.pi[:, :], 15, None, OP.bitwise_and))
+    vw()
+    v(V.tensor_copy(T.s0[:, :], T.pm[:, :]))
+    for a in range(4):
+        q = slice(32 * a, 32 * a + 32)
+        v(V.tensor_scalar(T.gsc[q, :], T.odd[q, :], -0.75 * 16.0 ** -a, 16.0 ** -a, OP.mult, OP.add))
+
+    A.wait_ge(S.ps, g_c)
+    for k in (256, 512, 1024):
+        k_s = s(A.activation(T.cwin[:, k:2 * k], T.cwin[:, 0:k], COPY))
+        A.wait_ge(S.s, k_s)
+
+    V.wait_ge(S.ld, 64)
+    v(V.tensor_copy(T.w16[0:64, :], T.wt[:, :]))
+    v_w = v(V.tensor_copy(T.w16[64:128, :], T.wt[:, :]))
+    vw()
+    v(V.tensor_copy(T.row[:, :], T.vwin[:, 0:2048].indirect(T.w16[:, 0:16])))
+    A.wait_ge(S.v, v_w)
+    s_cr = s(A.activation(T.crow[:, 0:256], T.cwin[:, 0:2048].indirect(T.w16[:, 0:16]), COPY))
+    A.wait_ge(S.ldx, 16)
+    for t in range(4):
+        s_xs = s(A.activation(T.xs[:, XW * t:XW * t + XW], T.xt[:, t:4 * XW:4], COPY))
+    vw()
+    v(V.transpose(T.rt[:, :], T.row[:, :]))
+    vw()
+    at = [0]
+    for b in range(8):
+        at.append(at[b] + 256 - 32 * b)
+    for b in range(8):
+        v(V.tensor_scalar(T.ne[:, at[b]:at[b + 1]], T.row[:, 32 * b:256], T.rt[:, 32 * b:32 * b + 1], None, OP.not_equal))
+    vw()
+    for b in range(8):
+        v(V.tensor_tensor_scan(T.sc[:, at[b]:at[b + 1]], T.ne[:, at[b]:at[b + 1]], T.ones[:, 0:256 - 32 * b], 0.0, OP.mult, OP.add))
+    vw()
+    V.wait_ge(S.ps, g_k)
+    for b in range(8):
+        v(V.tensor_scalar(T.fr[:, 32 * b:32 * b + 32], T.cst[:, 32 * b:32 * b + 32], T.sc[:, at[b + 1] - 1:at[b + 1]],
+                          T.rt[:, 32 * b:32 * b + 1], OP.is_equal, OP.mult))
+    vw()
+    v(V.transpose(T.qf[:, :], T.fr[:, :]))
+    vw()
+    v(V.tensor_scalar(T.ge[:, :], T.qf[:, :], T.gsc[:, 0:1], 128.0, OP.mult, OP.is_ge))
+    v(V.tensor_scalar(T.gh[:, :], T.qf[:, :], T.gsc[:, 0:1], 512.0, OP.mult, OP.is_ge))
+    vw()
+    v(V.tensor_tensor_scan(T.cc[:, :], T.ge[:, :], T.gh[:, :], 0.0, OP.add, OP.subtract))
+    vw()
+    for k in range(2):
+        v(V.tensor_scalar(T.le[:, 256 * k:256 * k + 256], T.cc[:, :], -16.0 * k, T.s0[:, 0:1], OP.add, OP.is_le))
+    vw()
+    for k in range(2):
+        v(V.tensor_tensor_scan(T.nn[:, 256 * k:256 * k + 256], T.ones[:, :], T.le[:, 256 * k:256 * k + 256], 0.0, OP.mult, OP.add))
+    vw()
+    for k in range(2):
+        v(V.tensor_scalar(T.jj[:, 2 * k:2 * k + 2], T.z2[:, :], T.nn[:, 256 * k + 255:256 * k + 256], None, OP.add))
+    vw()
+    V.wait_ge(S.s, s_cr)
+    v(V.tensor_copy(T.lg[:, :], T.crow[:, 0:272].indirect(T.jj[:, 0:4])))
+    vw()
+    v(V.transpose(T.lt[:, :], T.lg[:, :]))
+    vw()
+    v_msg = v(V.tensor_copy(T.msg[:, :], T.lt[:, 0:64:16]))
+    vw()
+
+    off = topo.engines(core, cores[others[0]])
+    on = [e for e in topo.engines(core, road[0][0]) if e not in off]
+    g.wait_ge(S.v, v_msg)
+    g.remote_dma_fused([xfer(topo, core, c, on[4 * i:4 * i + 4], S.rl, T.msg[:, 0:4], T.rl[:, 0:4])
+                        for i, (c, _) in enumerate(road)], local_sem=S.loc)
+
+    def among(f):
+        return [k for k in plane if k != f].index(r)
+    g.remote_dma_fused([xfer(topo, core, cores[f], off[2 * i:2 * i + 2], S.aa, T.msg[:, 0:4], T.la[:, 4 * among(f):4 * among(f) + 4])
+                        for i, f in enumerate(others)], local_sem=S.loc)
+    ps(g.iota(T.nb[:, :], [[512, 4], [0, 2], [256, 2]], 0, 0, **small))
+    ps(g.iota(T.dd[:, :], [[-448, 4], [32, 2], [-240, 2]], 1792, 1, **small))
+    col = [32 * (plane.index(k) if k in plane else 4 + far.index(k)) for k in range(8)]
+    vals = [col[2 * (m // 4) + m % 2] + 16 * (m // 2 % 2) for m in range(16)]
+    step = vals[1] - vals[0]
+    assert vals == [vals[0] + 16 * (m // 2) + step * (m % 2) for m in range(16)]
+    g_all = ps(g.iota(T.vp[:, :], [[16, 8], [step, 2], [1, 16]], vals[0], 0, **small))
+
+    oq, odd = r // 2, r % 2
+    mq = slice(32 * oq, 32 * oq + 32)
+    for a in range(4):
+        v(V.tensor_copy(T.oa[32 * a:32 * a + 32, 0:2], T.msg[mq, odd:4:2]))
+    V.wait_ge(S.ldw, 16)
+    v_qw = v(V.quantize_mx(T.qw[:, :], T.pw[:, :], T.wb[:, :]))
+    for b in range(4):
+        for a in range(4):
+            v(V.tensor_copy(T.ua[32 * a:32 * a + 32, 4 * b:4 * b + 4], T.msg[32 * b:32 * b + 32, :]))
+
+    def serve(lists, wide, offs, o0, tile, codes, plane8, sem, arrivals):
+        V.wait_ge(sem, arrivals)
+        for a in range(4):
+            v_o = v(V.tensor_copy(offs[32 * a:32 * a + 32, o0:8], lists[mq, odd:wide:2]))
+        vw()
+        for t in range(2):
+            v(V.tensor_copy(tile[:, t:512:4], T.xs[:, XW * t:XW * t + XW].indirect(offs[:, 0:8])))
+        A.wait_ge(S.v, v_o)
+        for t in range(2, 4):
+            s_t = s(A.activation(tile[:, t:512:4], T.xs[:, XW * t:XW * t + XW].indirect(offs[:, 0:8]), COPY))
+        vw()
+        V.wait_ge(S.s, s_t)
+        return v(V.quantize_mx(codes[:, :], plane8[:, :], tile[:, :]))
+
+    V.wait_ge(S.s, s_xs)
+    A.wait_ge(S.s, s_xs)
+    v_qa = serve(T.la, 12, T.oa, 2, T.ta, T.qa, T.pa, S.aa, 6)
+    v_qb = serve(T.lb, 16, T.ob, 0, T.tb, T.qb, T.pb, S.ab, 16)
+
+    g.wait_ge(S.v, v_qa)
+    g.remote_dma_fused([xfer(topo, core, cores[f], off[2 * i:2 * i + 2], S.ac, u8(T.qa[:, 32 + 32 * i:64 + 32 * i]),
+                             u8(T.ca[:, 32 * me:32 * me + 32])) for i, f in enumerate(others)], local_sem=S.loc)
+    g.remote_dma_fused([xfer(topo, core, cores[f], off[2 * i:2 * i + 2], S.ac, T.pa[:, 32 + 32 * i:64 + 32 * i],
+                             T.da[:, 32 * me:32 * me + 32]) for i, f in enumerate(others)], local_sem=S.loc)
+    g.wait_ge(S.v, v_qb)
+    g.remote_dma_fused([xfer(topo, core, c, on[4 * i:4 * i + 4], S.rc, u8(T.qb[:, 64 * i:64 * i + 64]), u8(T.rc[:, :]))
+                        for i, (c, _) in enumerate(road)], local_sem=S.loc)
+    g.remote_dma_fused([xfer(topo, core, c, on[4 * i:4 * i + 4], S.rs, T.pb[:, 64 * i:64 * i + 64], T.rs[:, :])
+                        for i, (c, _) in enumerate(road)], local_sem=S.loc)
+    g.wait_ge(S.loc, 3 * 8 + 3 * 6)
+    D.wait_ge(S.v, v_qa)
+    D.dma_start(u8(T.ca[:, 32 * me:32 * me + 32]), u8(T.qa[:, 0:32])).then_inc(S.own, 16)
+    D.dma_start(T.da[:, 32 * me:32 * me + 32], T.pa[:, 0:32]).then_inc(S.own, 16)
+
+    V.wait_ge(S.ps, g_all)
+    v(V.tensor_scalar(T.fu[:, :], T.ua[:, :], 256.0, None, OP.is_ge))
+    v(V.tensor_tensor(T.u2[:, :], T.ua[:, :], T.nb[:, :], OP.add))
+    v(V.tensor_copy(T.w2[:, 0:32:2], T.w16[:, :]))
+    v(V.tensor_copy(T.w2[:, 1:32:2], T.w16[:, :]))
+    vw()
+    v(V.tensor_tensor(T.u1[:, :], T.fu[:, :], T.dd[:, :], OP.mult))
+    vw()
+    v(V.tensor_tensor(T.u3[:, :], T.u1[:, :], T.u2[:, :], OP.add))
+    vw()
+    v(V.tensor_copy(T.ou[:, :], T.u3[:, :]))
+    vw()
+    v(V.tensor_copy(T.vwin[:, 0:PW].indirect(T.ou[:, 0:16]), T.vp[:, :]))
+    vw()
+    v(V.tensor_copy(T.pr[:, :], T.vwin[:, 0:2048].indirect(T.w2[:, 0:32])))
+    vw()
+    v(V.transpose(T.pt[:, :], T.pr[:, :]))
+    vw()
+    v_oy = v(V.tensor_copy(T.oy[:, :], T.pt[:, 0:512:32]))
+
+    P.wait_ge(S.v, v_qw)
+    P.wait_ge(S.ac, 12)
+    P.wait_ge(S.own, 32)
+    P.matmul_mx(T.m0[:, 0:128], T.qw[:, :], T.pw[:, :], T.ca[:, :], T.da[:, :], True, True).then_inc(S.te, 1)
+    P.wait_ge(S.ad, 32)
+    P.matmul_mx(T.m1[:, 0:128], T.qw[:, :], T.pw[:, :], T.cb[:, :], T.db[:, :], True, True).then_inc(S.te, 1)
+    A.wait_ge(S.te, 1)
+    s_y = s(A.activation(T.ys[:, 0:128], T.m0[:, 0:128], COPY))
+    V.wait_ge(S.te, 2)
+    v_y = v(V.tensor_copy(T.ys[:, 128:256], T.m1[:, 0:128]))
+    vw()
+    V.wait_ge(S.s, s_y)
+    v_o = v(V.tensor_copy(T.yo[:, 0:128], T.ys[:, 0:256].indirect(T.oy[:, 0:8])))
+    A.wait_ge(S.v, v_y)
+    A.wait_ge(S.s, s_y)
+    s_o = s(A.activation(T.yo[:, 128:256], T.ys[:, 0:256].indirect(T.oy[:, 8:16]), COPY))
+    D.wait_ge(S.v, v_o)
+    D.dma_start(T.y[:, 0:128], T.yo[:, 0:128]).then_inc(S.st, 16)
+    A.wait_ge(S.s, s_o)
+    A.dma_start(T.y[:, 128:256], T.yo[:, 128:256]).then_inc(S.su, 16)
+    D.wait_ge(S.st, 16)
+    A.wait_ge(S.su, 16)

@@ -5,20 +5,22 @@ OP = AluOpType
 COPY = ActivationFunctionType.Copy
 XW = 272
 PW = 2432
+SMALL = {"allow_small_or_imprecise_dtypes": True}
 
-SCRATCH = {"wt": ("sbuf", [64, 16], "int32"), "m0": ("psum", [128, 512], "float32"), "m1": ("psum", [128, 512], "float32")}
-for _t, _b in (("int32", "pi 1 pm 1 odd 1"),
-               ("uint16", "w16 16 w2 32 jj 4 msg 4 la 12 lb 16 oa 8 ob 8 rl 4 ou 16 oy 16"),
-               ("float32", "z2 2 s0 1 gsc 1 ua 16 fu 16 u1 16 u2 16 u3 16 nb 16 dd 16 ys 256 yo 256"),
-               ("bfloat16", "vwin %d cwin 2048 ones 256 cst 256 row 256 crow 272 rt 256 ne 1152 sc 1152 fr 256 qf 256 "
-                            "ge 256 gh 256 cc 256 le 512 nn 512 lg 64 lt 64 xt %d xs %d wb 512 ta 512 tb 512 vp 256 "
-                            "pr 512 pt 512" % (PW, 4 * XW, 4 * XW)),
+SCRATCH = {"wt": ("sbuf", [64, 16], "int32"), "hw": ("dram", [128, 2], "int32"),
+           "m0": ("psum", [128, 512], "float32"), "m1": ("psum", [128, 512], "float32")}
+for _t, _b in (("int32", "pi 1 pm 1 odd 1 w0 2"),
+               ("uint16", "w16 16 w2 32 jj 4 msg 4 la 6 lb 8 oa 8 ob 8 rl 4 ou 16 oy 16"),
+               ("float32", "z2 2 k0 1 s0 1 s1 1 gsc 1 ua 16 fu 16 u1 16 u2 16 u3 16 nb 16 dd 16 ys 256 yo 256"),
+               ("bfloat16", "vwin 2048 pos %d cwin 2048 ones 256 cst 128 row 256 crow 272 rt 128 ne 832 sc 832 fr 128 "
+                            "qf 256 ge 256 gh 256 cc 256 le 512 nn 512 lg 64 lt 64 xt %d xs %d wb 512 ta 512 tb 512 "
+                            "vp 256 pr 512 pt 512" % (PW, 4 * XW, 4 * XW)),
                ("float8_e4m3fn_x4", "qw 128 qa 128 qb 128 ca 128 cb 128 rc 64"),
                ("uint8", "pw 128 pa 128 pb 128 da 128 db 128 rs 64")):
     _w = _b.split()
     for _i in range(0, len(_w), 2):
         SCRATCH[_w[_i]] = ("sbuf", [128, int(_w[_i + 1])], _t)
-SEMAPHORES = "ld ldx ldw v s ps te aa ab ac ad own st su loc rl rc rs".split()
+SEMAPHORES = "ld ldx ldw ld0 v s ps te aa ab ac ad own st su loc rl rc rs th hs oy".split()
 
 
 def plane_of(topo, cores, r):
@@ -35,9 +37,13 @@ def roads(topo, cores, r):
     return [(pair[h], [f for b, f in enumerate(far) if (a + b) % 2 == h]) for h in range(2)]
 
 
+def mask(engines):
+    return sum(1 << k for k in engines)
+
+
 def xfer(topo, src_core, dst_core, engines, sem, src, dst):
     rid, pid = topo.addr(dst_core, src_core)
-    return RemoteDMATransfer(dst_ids=[DstId(rid=rid, pnc=pid)], dma_engine_mask=sum(1 << k for k in engines),
+    return RemoteDMATransfer(dst_ids=[DstId(rid=rid, pnc=pid)], dma_engine_mask=mask(engines),
                              remote_sem=sem, srcs=[src], dsts=[dst], alu_op=0)
 
 
@@ -45,24 +51,85 @@ def u8(view):
     return view.bitcast(dt.uint8)
 
 
-def relay(g, core, T, topo, r, ranks):
+def relay(g, core, T, topo, r, h, ranks):
     cores = T.cores
-    me = plane_of(topo, cores, r).index(r)
     en = topo.engines(core, cores[ranks[0]])
     half = [en[0:len(en) // 2], en[len(en) // 2:]]
+    plane = plane_of(topo, cores, r)
+    far = [k for k in range(len(cores)) if k not in plane]
+    rid, pid = topo.addr(cores[r], core)
+    V, D, S = g.vector, g.sync, T.sem
+    n = [0]
+
+    def v(call):
+        call.then_inc(S.v, 1)
+        n[0] += 1
+
+    def vw():
+        V.wait_ge(S.v, n[0])
+    g.iota(T.pi[:, 0:1], [[0, 1]], 0, 1).then_inc(S.ps, 1)
+    V.wait_ge(S.ps, 1)
+    v(V.tensor_scalar(T.pm[:, :], T.pi[:, :], 15, None, OP.bitwise_and))
+    vw()
+    v(V.tensor_scalar(T.k0[:, :], T.pm[:, :], 16.0 * h, None, OP.add))
+    g.wait_ge(S.v, n[0])
+    g.remote_dma(T["s%d" % h][:, 0:1], T.k0[:, 0:1], S.th, S.loc, pid, rid, mask(en))
+    if h == 0:
+        D.wait_ge(S.hs, 8)
+        for i in range(4):
+            D.dma_start(T.wt[16 * i:16 * i + 16, :], T.hw[:, :]).then_inc(S.ld, 16)
+        g.iota(T.nb[:, :], [[256, 8], [0, 2]], 0, 0, **SMALL).then_inc(S.ps, 1)
+        g.iota(T.dd[:, :], [[-224, 8], [16, 2]], 1792, 1, **SMALL).then_inc(S.ps, 1)
+        col = [32 * (plane.index(k) if k in plane else 4 + far.index(k)) for k in range(8)]
+        step = col[1] - col[0]
+        assert col == [col[0] + 32 * (k // 2) + step * (k % 2) for k in range(8)]
+        g.iota(T.vp[:, :], [[32, 4], [step, 2], [1, 32]], col[0], 0, **SMALL).then_inc(S.ps, 1)
+        v(V.memset(T.pos[:, 0:2048], 0.0))
+        V.wait_ge(S.ld, 64)
+        v(V.tensor_copy(T.w16[0:64, :], T.wt[:, :]))
+        v(V.tensor_copy(T.w16[64:128, :], T.wt[:, :]))
+        vw()
+        v(V.tensor_copy(T.w2[:, 0:32:2], T.w16[:, :]))
+        v(V.tensor_copy(T.w2[:, 1:32:2], T.w16[:, :]))
+        V.wait_ge(S.ps, 4)
+        V.wait_ge(S.rl, 4)
+        for b in range(4):
+            for a in range(4):
+                v(V.tensor_copy(T.ua[32 * a:32 * a + 32, 4 * b:4 * b + 4], T.rl[32 * b:32 * b + 32, :]))
+        vw()
+        v(V.tensor_scalar(T.fu[:, :], T.ua[:, :], 256.0, None, OP.is_ge))
+        v(V.tensor_tensor(T.u2[:, :], T.ua[:, :], T.nb[:, :], OP.add))
+        vw()
+        v(V.tensor_tensor(T.u1[:, :], T.fu[:, :], T.dd[:, :], OP.mult))
+        vw()
+        v(V.tensor_tensor(T.u3[:, :], T.u1[:, :], T.u2[:, :], OP.add))
+        vw()
+        v(V.tensor_copy(T.ou[:, :], T.u3[:, :]))
+        vw()
+        v(V.tensor_copy(T.pos[:, 0:PW].indirect(T.ou[:, 0:16]), T.vp[:, :]))
+        vw()
+        v(V.tensor_copy(T.pr[:, :], T.pos[:, 0:2048].indirect(T.w2[:, 0:32])))
+        vw()
+        v(V.transpose(T.pt[:, :], T.pr[:, :]))
+        vw()
+        v(V.tensor_copy(T.oy[:, :], T.pt[:, 0:512:32]))
 
     def place(f):
-        return [k for _, ks in roads(topo, cores, f) for k in ks].index(r)
-    g.wait_ge(T.sem.rl, 4)
-    g.remote_dma_fused([xfer(topo, core, cores[f], half[i], T.sem.ab, T.rl[:, 0:4], T.lb[:, 4 * place(f):4 * place(f) + 4])
-                        for i, f in enumerate(ranks)], local_sem=T.sem.loc)
-    g.wait_ge(T.sem.rc, 4)
-    g.remote_dma_fused([xfer(topo, core, cores[f], half[i], T.sem.ad, u8(T.rc[:, 32 * i:32 * i + 32]),
-                             u8(T.cb[:, 32 * me:32 * me + 32])) for i, f in enumerate(ranks)], local_sem=T.sem.loc)
-    g.wait_ge(T.sem.rs, 4)
-    g.remote_dma_fused([xfer(topo, core, cores[f], half[i], T.sem.ad, T.rs[:, 32 * i:32 * i + 32],
-                             T.db[:, 32 * me:32 * me + 32]) for i, f in enumerate(ranks)], local_sem=T.sem.loc)
-    g.wait_ge(T.sem.loc, 3 * len(en))
+        return 2 * [k for _, ks in roads(topo, cores, f) for k in ks].index(r)
+    g.wait_ge(S.rl, 4)
+    g.remote_dma_fused([xfer(topo, core, cores[f], half[i], S.ab, T.rl[:, 2 * (f % 2):2 * (f % 2) + 2],
+                             T.lb[:, place(f):place(f) + 2]) for i, f in enumerate(ranks)], local_sem=S.loc)
+    if h == 0:
+        g.wait_ge(S.v, n[0])
+        g.remote_dma(T.oy[:, 0:16], T.oy[:, 0:16], S.oy, S.loc, pid, rid, mask(en))
+    here = slice(32 * plane.index(r), 32 * plane.index(r) + 32)
+    g.wait_ge(S.rc, 4)
+    g.remote_dma_fused([xfer(topo, core, cores[f], half[i], S.ad, u8(T.rc[:, 32 * i:32 * i + 32]), u8(T.cb[:, here]))
+                        for i, f in enumerate(ranks)], local_sem=S.loc)
+    g.wait_ge(S.rs, 4)
+    g.remote_dma_fused([xfer(topo, core, cores[f], half[i], S.ad, T.rs[:, 32 * i:32 * i + 32], T.db[:, here])
+                        for i, f in enumerate(ranks)], local_sem=S.loc)
+    g.wait_ge(S.loc, (5 - h) * len(en))
 
 
 def rank_program(g, core, T, topo):
@@ -71,16 +138,18 @@ def rank_program(g, core, T, topo):
     if r is None:
         for k in range(len(cores)):
             if core in topo.cores_of(cores[k]):
-                for c, ranks in roads(topo, cores, k):
+                for h, (c, ranks) in enumerate(roads(topo, cores, k)):
                     if c == core:
-                        relay(g, core, T, topo, k, ranks)
+                        relay(g, core, T, topo, k, h, ranks)
         return
     S = T.sem
     plane = plane_of(topo, cores, r)
     others = [k for k in plane if k != r]
     road = roads(topo, cores, r)
-    far = [k for k in range(len(cores)) if k not in plane]
     me = plane.index(r)
+    h_rid, h_pid = topo.addr(road[0][0], core)
+    off = topo.engines(core, cores[others[0]])
+    on = [e for e in topo.engines(core, road[0][0]) if e not in off]
     V, A, D, P = g.vector, g.scalar, g.sync, g.tensor
     n = {"v": 0, "s": 0, "ps": 0}
 
@@ -105,34 +174,33 @@ def rank_program(g, core, T, topo):
     A.dma_start(T.wt[16:32, :], T.want[:, :]).then_inc(S.ld, 16)
     D.dma_start(T.wt[32:48, :], T.want[:, :]).then_inc(S.ld, 16)
     A.dma_start(T.wt[48:64, :], T.want[:, :]).then_inc(S.ld, 16)
+    A.dma_start(T.w0[:, :], T.want[:, :]).then_inc(S.ld0, 16)
     D.dma_start(T.xt[:, 0:1024], T.x[:, :]).then_inc(S.ldx, 16)
     D.dma_start(T.wb[:, :], T.w[:, :]).then_inc(S.ldw, 16)
 
-    small = {"allow_small_or_imprecise_dtypes": True}
-    g_v = ps(g.iota(T.vwin[:, 0:128], [[1, 128]], 128, 0, **small))
-    g_c = ps(g.iota(T.cwin[:, 0:256], [[1, 256]], 0, 0, **small))
     g_p = ps(g.iota(T.pi[:, 0:1], [[0, 1]], 0, 1))
+    g_v = ps(g.iota(T.vwin[:, 0:128], [[1, 128]], 128, 0, **SMALL))
+    g_c = ps(g.iota(T.cwin[:, 0:256], [[1, 256]], 0, 0, **SMALL))
     for a in range(4):
         g.wait_ge(S.ps, n["ps"])
-        g_k = ps(g.iota(T.cst[32 * a:32 * a + 32, 0:256], [[-32, 8], [0, 32]], 256, -1, **small))
-    g.wait_ge(S.ps, g_k)
+        g_k = ps(g.iota(T.cst[32 * a:32 * a + 32, 0:128], [[-32, 4], [0, 32]], 256 - 128 * (a // 2), -1, **SMALL))
+    g.wait_ge(S.ld0, 16)
+    g.remote_dma(T.hw[:, :], T.w0[:, 0:2], S.hs, S.loc, h_pid, h_rid, mask(on))
 
     v(V.memset(T.ones[:, :], 1.0))
     v(V.memset(T.crow[:, 256:272], 256.0))
     v(V.memset(T.xt[:, 1024:4 * XW], 0.0))
     v(V.memset(T.z2[:, :], 0.0))
-    V.wait_ge(S.ps, g_v)
-    for k, f in ((128, 2.0), (256, 4.0), (512, 16.0), (1024, 256.0)):
-        v_k = v(V.tensor_scalar(T.vwin[:, k:2 * k], T.vwin[:, 0:k], f, None, OP.mult))
-        vw()
     V.wait_ge(S.ps, g_p)
     v(V.tensor_scalar(T.odd[:, :], T.pi[:, :], 4, 1, OP.arith_shift_right, OP.bitwise_and))
-    v(V.tensor_scalar(T.pm[:, :], T.pi[:, :], 15, None, OP.bitwise_and))
     vw()
-    v(V.tensor_copy(T.s0[:, :], T.pm[:, :]))
     for a in range(4):
         q = slice(32 * a, 32 * a + 32)
         v(V.tensor_scalar(T.gsc[q, :], T.odd[q, :], -0.75 * 16.0 ** -a, 16.0 ** -a, OP.mult, OP.add))
+    V.wait_ge(S.ps, g_v)
+    for k, f in ((128, 2.0), (256, 4.0), (512, 16.0), (1024, 256.0)):
+        v(V.tensor_scalar(T.vwin[:, k:2 * k], T.vwin[:, 0:k], f, None, OP.mult))
+        vw()
 
     A.wait_ge(S.ps, g_c)
     for k in (256, 512, 1024):
@@ -150,31 +218,38 @@ def rank_program(g, core, T, topo):
     for t in range(4):
         s_xs = s(A.activation(T.xs[:, XW * t:XW * t + XW], T.xt[:, t:4 * XW:4], COPY))
     vw()
-    v(V.transpose(T.rt[:, :], T.row[:, :]))
+    halves = [slice(64 * h, 64 * h + 64) for h in range(2)]
+    for h in range(2):
+        v(V.transpose(T.rt[halves[h], 0:128], T.row[halves[h], 128 * h:128 * h + 128]))
     vw()
     at = [0]
-    for b in range(8):
+    for b in range(4):
         at.append(at[b] + 256 - 32 * b)
-    for b in range(8):
+    for b in range(4):
         v(V.tensor_scalar(T.ne[:, at[b]:at[b + 1]], T.row[:, 32 * b:256], T.rt[:, 32 * b:32 * b + 1], None, OP.not_equal))
     vw()
-    for b in range(8):
+    for b in range(4):
         v(V.tensor_tensor_scan(T.sc[:, at[b]:at[b + 1]], T.ne[:, at[b]:at[b + 1]], T.ones[:, 0:256 - 32 * b], 0.0, OP.mult, OP.add))
     vw()
     V.wait_ge(S.ps, g_k)
-    for b in range(8):
+    for b in range(4):
         v(V.tensor_scalar(T.fr[:, 32 * b:32 * b + 32], T.cst[:, 32 * b:32 * b + 32], T.sc[:, at[b + 1] - 1:at[b + 1]],
                           T.rt[:, 32 * b:32 * b + 1], OP.is_equal, OP.mult))
     vw()
-    v(V.transpose(T.qf[:, :], T.fr[:, :]))
+    for h in range(2):
+        v(V.transpose(T.qf[halves[h], 128 * h:128 * h + 128], T.fr[halves[h], 0:128]))
+    vw()
+    for h in range(2):
+        v(V.tensor_copy(T.qf[halves[1 - h], 128 * h:128 * h + 128], T.qf[halves[h], 128 * h:128 * h + 128]))
     vw()
     v(V.tensor_scalar(T.ge[:, :], T.qf[:, :], T.gsc[:, 0:1], 128.0, OP.mult, OP.is_ge))
     v(V.tensor_scalar(T.gh[:, :], T.qf[:, :], T.gsc[:, 0:1], 512.0, OP.mult, OP.is_ge))
     vw()
     v(V.tensor_tensor_scan(T.cc[:, :], T.ge[:, :], T.gh[:, :], 0.0, OP.add, OP.subtract))
     vw()
+    V.wait_ge(S.th, 16)
     for k in range(2):
-        v(V.tensor_scalar(T.le[:, 256 * k:256 * k + 256], T.cc[:, :], -16.0 * k, T.s0[:, 0:1], OP.add, OP.is_le))
+        v(V.tensor_scalar(T.le[:, 256 * k:256 * k + 256], T.cc[:, :], T["s%d" % k][:, 0:1], None, OP.is_le))
     vw()
     for k in range(2):
         v(V.tensor_tensor_scan(T.nn[:, 256 * k:256 * k + 256], T.ones[:, :], T.le[:, 256 * k:256 * k + 256], 0.0, OP.mult, OP.add))
@@ -187,41 +262,29 @@ def rank_program(g, core, T, topo):
     vw()
     v(V.transpose(T.lt[:, :], T.lg[:, :]))
     vw()
-    v_msg = v(V.tensor_copy(T.msg[:, :], T.lt[:, 0:64:16]))
+    for k in range(2):
+        v_msg = v(V.tensor_copy(T.msg[:, 2 * k:2 * k + 2], T.lt[:, 16 * k:64:32]))
     vw()
 
-    off = topo.engines(core, cores[others[0]])
-    on = [e for e in topo.engines(core, road[0][0]) if e not in off]
     g.wait_ge(S.v, v_msg)
     g.remote_dma_fused([xfer(topo, core, c, on[4 * i:4 * i + 4], S.rl, T.msg[:, 0:4], T.rl[:, 0:4])
                         for i, (c, _) in enumerate(road)], local_sem=S.loc)
 
     def among(f):
-        return [k for k in plane if k != f].index(r)
-    g.remote_dma_fused([xfer(topo, core, cores[f], off[2 * i:2 * i + 2], S.aa, T.msg[:, 0:4], T.la[:, 4 * among(f):4 * among(f) + 4])
-                        for i, f in enumerate(others)], local_sem=S.loc)
-    ps(g.iota(T.nb[:, :], [[512, 4], [0, 2], [256, 2]], 0, 0, **small))
-    ps(g.iota(T.dd[:, :], [[-448, 4], [32, 2], [-240, 2]], 1792, 1, **small))
-    col = [32 * (plane.index(k) if k in plane else 4 + far.index(k)) for k in range(8)]
-    vals = [col[2 * (m // 4) + m % 2] + 16 * (m // 2 % 2) for m in range(16)]
-    step = vals[1] - vals[0]
-    assert vals == [vals[0] + 16 * (m // 2) + step * (m % 2) for m in range(16)]
-    g_all = ps(g.iota(T.vp[:, :], [[16, 8], [step, 2], [1, 16]], vals[0], 0, **small))
+        return 2 * [k for k in plane if k != f].index(r)
+    g.remote_dma_fused([xfer(topo, core, cores[f], off[2 * i:2 * i + 2], S.aa, T.msg[:, 2 * (f % 2):2 * (f % 2) + 2],
+                             T.la[:, among(f):among(f) + 2]) for i, f in enumerate(others)], local_sem=S.loc)
 
-    oq, odd = r // 2, r % 2
-    mq = slice(32 * oq, 32 * oq + 32)
+    mq = slice(32 * (r // 2), 32 * (r // 2) + 32)
     for a in range(4):
-        v(V.tensor_copy(T.oa[32 * a:32 * a + 32, 0:2], T.msg[mq, odd:4:2]))
+        v(V.tensor_copy(T.oa[32 * a:32 * a + 32, 0:2], T.msg[mq, 2 * (r % 2):2 * (r % 2) + 2]))
     V.wait_ge(S.ldw, 16)
     v_qw = v(V.quantize_mx(T.qw[:, :], T.pw[:, :], T.wb[:, :]))
-    for b in range(4):
-        for a in range(4):
-            v(V.tensor_copy(T.ua[32 * a:32 * a + 32, 4 * b:4 * b + 4], T.msg[32 * b:32 * b + 32, :]))
 
-    def serve(lists, wide, offs, o0, tile, codes, plane8, sem, arrivals):
+    def serve(lists, offs, o0, tile, codes, plane8, sem, arrivals):
         V.wait_ge(sem, arrivals)
         for a in range(4):
-            v_o = v(V.tensor_copy(offs[32 * a:32 * a + 32, o0:8], lists[mq, odd:wide:2]))
+            v_o = v(V.tensor_copy(offs[32 * a:32 * a + 32, o0:8], lists[mq, :]))
         vw()
         for t in range(2):
             v(V.tensor_copy(tile[:, t:512:4], T.xs[:, XW * t:XW * t + XW].indirect(offs[:, 0:8])))
@@ -234,43 +297,24 @@ def rank_program(g, core, T, topo):
 
     V.wait_ge(S.s, s_xs)
     A.wait_ge(S.s, s_xs)
-    v_qa = serve(T.la, 12, T.oa, 2, T.ta, T.qa, T.pa, S.aa, 6)
-    v_qb = serve(T.lb, 16, T.ob, 0, T.tb, T.qb, T.pb, S.ab, 16)
+    v_qa = serve(T.la, T.oa, 2, T.ta, T.qa, T.pa, S.aa, 6)
+    v_qb = serve(T.lb, T.ob, 0, T.tb, T.qb, T.pb, S.ab, 16)
 
+    here = slice(32 * me, 32 * me + 32)
     g.wait_ge(S.v, v_qa)
     g.remote_dma_fused([xfer(topo, core, cores[f], off[2 * i:2 * i + 2], S.ac, u8(T.qa[:, 32 + 32 * i:64 + 32 * i]),
-                             u8(T.ca[:, 32 * me:32 * me + 32])) for i, f in enumerate(others)], local_sem=S.loc)
+                             u8(T.ca[:, here])) for i, f in enumerate(others)], local_sem=S.loc)
     g.remote_dma_fused([xfer(topo, core, cores[f], off[2 * i:2 * i + 2], S.ac, T.pa[:, 32 + 32 * i:64 + 32 * i],
-                             T.da[:, 32 * me:32 * me + 32]) for i, f in enumerate(others)], local_sem=S.loc)
+                             T.da[:, here]) for i, f in enumerate(others)], local_sem=S.loc)
     g.wait_ge(S.v, v_qb)
     g.remote_dma_fused([xfer(topo, core, c, on[4 * i:4 * i + 4], S.rc, u8(T.qb[:, 64 * i:64 * i + 64]), u8(T.rc[:, :]))
                         for i, (c, _) in enumerate(road)], local_sem=S.loc)
     g.remote_dma_fused([xfer(topo, core, c, on[4 * i:4 * i + 4], S.rs, T.pb[:, 64 * i:64 * i + 64], T.rs[:, :])
                         for i, (c, _) in enumerate(road)], local_sem=S.loc)
-    g.wait_ge(S.loc, 3 * 8 + 3 * 6)
+    g.wait_ge(S.loc, 8 + 3 * 8 + 3 * 6)
     D.wait_ge(S.v, v_qa)
-    D.dma_start(u8(T.ca[:, 32 * me:32 * me + 32]), u8(T.qa[:, 0:32])).then_inc(S.own, 16)
-    D.dma_start(T.da[:, 32 * me:32 * me + 32], T.pa[:, 0:32]).then_inc(S.own, 16)
-
-    V.wait_ge(S.ps, g_all)
-    v(V.tensor_scalar(T.fu[:, :], T.ua[:, :], 256.0, None, OP.is_ge))
-    v(V.tensor_tensor(T.u2[:, :], T.ua[:, :], T.nb[:, :], OP.add))
-    v(V.tensor_copy(T.w2[:, 0:32:2], T.w16[:, :]))
-    v(V.tensor_copy(T.w2[:, 1:32:2], T.w16[:, :]))
-    vw()
-    v(V.tensor_tensor(T.u1[:, :], T.fu[:, :], T.dd[:, :], OP.mult))
-    vw()
-    v(V.tensor_tensor(T.u3[:, :], T.u1[:, :], T.u2[:, :], OP.add))
-    vw()
-    v(V.tensor_copy(T.ou[:, :], T.u3[:, :]))
-    vw()
-    v(V.tensor_copy(T.vwin[:, 0:PW].indirect(T.ou[:, 0:16]), T.vp[:, :]))
-    vw()
-    v(V.tensor_copy(T.pr[:, :], T.vwin[:, 0:2048].indirect(T.w2[:, 0:32])))
-    vw()
-    v(V.transpose(T.pt[:, :], T.pr[:, :]))
-    vw()
-    v_oy = v(V.tensor_copy(T.oy[:, :], T.pt[:, 0:512:32]))
+    D.dma_start(u8(T.ca[:, here]), u8(T.qa[:, 0:32])).then_inc(S.own, 16)
+    D.dma_start(T.da[:, here], T.pa[:, 0:32]).then_inc(S.own, 16)
 
     P.wait_ge(S.v, v_qw)
     P.wait_ge(S.ac, 12)
@@ -280,6 +324,8 @@ def rank_program(g, core, T, topo):
     P.matmul_mx(T.m1[:, 0:128], T.qw[:, :], T.pw[:, :], T.cb[:, :], T.db[:, :], True, True).then_inc(S.te, 1)
     A.wait_ge(S.te, 1)
     s_y = s(A.activation(T.ys[:, 0:128], T.m0[:, 0:128], COPY))
+    V.wait_ge(S.oy, 8)
+    A.wait_ge(S.oy, 8)
     V.wait_ge(S.te, 2)
     v_y = v(V.tensor_copy(T.ys[:, 128:256], T.m1[:, 0:128]))
     vw()

@@ -10,17 +10,17 @@ SMALL = {"allow_small_or_imprecise_dtypes": True}
 SCRATCH = {"wt": ("sbuf", [64, 16], "int32"), "hw": ("dram", [128, 2], "int32"),
            "m0": ("psum", [128, 512], "float32"), "m1": ("psum", [128, 512], "float32")}
 for _t, _b in (("int32", "pi 1 pm 1 odd 1 w0 2"),
-               ("uint16", "w16 16 w2 32 jj 4 msg 4 la 6 lb 8 oa 8 ob 8 rl 4 ou 16 oy 16"),
-               ("float32", "z2 2 k0 1 s0 1 s1 1 gsc 1 ua 16 fu 16 u1 16 u2 16 u3 16 nb 16 dd 16 ys 256 yo 256"),
-               ("bfloat16", "vwin 2048 pos %d cwin 2048 ones 256 cst 128 row 256 crow 272 rt 128 ne 832 sc 832 fr 128 "
-                            "qf 256 ge 256 gh 256 cc 256 le 512 nn 512 lg 64 lt 64 xt %d xs %d wb 512 ta 512 tb 512 "
-                            "vp 256 pr 512 pt 512" % (PW, 4 * XW, 4 * XW)),
-               ("float8_e4m3fn_x4", "qw 128 qa 128 qb 128 ca 128 cb 128 rc 64"),
-               ("uint8", "pw 128 pa 128 pb 128 da 128 db 128 rs 64")):
+               ("uint16", "w16 16 w2 32 jj 4 msg 4 la 6 lb 8 oa 8 ob 8 rl 2 rp 4 ou 16 oy 16"),
+               ("float32", "gsc 1 ua 16 fu 16 u1 16 u2 16 u3 16 nb 16 dd 16 ys 256 yo 256"),
+               ("bfloat16", "k0 2 z2 2 s0 1 s1 1 vwin 2048 pos %d cwin 2048 ones 256 cst 128 row 256 crow 272 rt 128 "
+                            "ne 832 sc 832 fr 128 qf 256 ge 256 gh 256 cc 256 le 512 nn 512 lg 64 lt 64 xt %d xs %d "
+                            "wb 512 ta 512 tb 512 vp 256 pr 512 pt 512" % (PW, 4 * XW, 4 * XW)),
+               ("float8_e4m3fn_x4", "qw 128 qa 128 qb 128 ca 128 cb 128 rc 32 ra 32"),
+               ("uint8", "pw 128 pa 128 pb 128 da 128 db 128 rs 32 rz 32")):
     _w = _b.split()
     for _i in range(0, len(_w), 2):
         SCRATCH[_w[_i]] = ("sbuf", [128, int(_w[_i + 1])], _t)
-SEMAPHORES = "ld ldx ldw ld0 v s ps te aa ab ac ad own st su loc rl rc rs th hs oy".split()
+SEMAPHORES = "ld ldx ldw ld0 v s ps te aa ab ac ad own st su loc rl rp rc rs ra rz th tz tc hs oy".split()
 
 
 def plane_of(topo, cores, r):
@@ -30,11 +30,12 @@ def plane_of(topo, cores, r):
 def roads(topo, cores, r):
     mine = plane_of(topo, cores, r)
     far = [k for k in range(len(cores)) if k not in mine]
+    near = [None] + [k for k in mine if k != r]
     c = cores[r]
     able = [k for k in topo.cores_of(c) if k != c and all(topo.may_write(k, cores[f]) for f in far)]
-    pair = [[k for k in able if topo.die(k) == topo.die(c)][0], [k for k in able if topo.die(k) != topo.die(c)][0]]
+    able = [k for k in able if topo.die(k) == topo.die(c)] + [k for k in able if topo.die(k) != topo.die(c)]
     a = mine.index(r)
-    return [(pair[h], [f for b, f in enumerate(far) if (a + b) % 2 == h]) for h in range(2)]
+    return [(able[h], far[(h - a) % len(far)], near[h]) for h in range(len(far))]
 
 
 def mask(engines):
@@ -51,15 +52,14 @@ def u8(view):
     return view.bitcast(dt.uint8)
 
 
-def relay(g, core, T, topo, r, h, ranks):
+def relay(g, core, T, topo, r, h, f, near):
     cores = T.cores
-    en = topo.engines(core, cores[ranks[0]])
-    half = [en[0:len(en) // 2], en[len(en) // 2:]]
+    en = topo.engines(core, cores[f])
     plane = plane_of(topo, cores, r)
     far = [k for k in range(len(cores)) if k not in plane]
-    rid, pid = topo.addr(cores[r], core)
     V, D, S = g.vector, g.sync, T.sem
     n = [0]
+    left = [0]
 
     def v(call):
         call.then_inc(S.v, 1)
@@ -67,15 +67,24 @@ def relay(g, core, T, topo, r, h, ranks):
 
     def vw():
         V.wait_ge(S.v, n[0])
-    g.iota(T.pi[:, 0:1], [[0, 1]], 0, 1).then_inc(S.ps, 1)
-    V.wait_ge(S.ps, 1)
-    v(V.tensor_scalar(T.pm[:, :], T.pi[:, :], 15, None, OP.bitwise_and))
-    vw()
-    v(V.tensor_scalar(T.k0[:, :], T.pm[:, :], 16.0 * h, None, OP.add))
+
+    def send(k, sem, src, dst):
+        rid, pid = topo.addr(cores[k], core)
+        g.remote_dma(dst, src, sem, S.loc, pid, rid, mask(en))
+        left[0] += len(en)
+    if h < 2:
+        g.iota(T.pi[:, 0:1], [[0, 1]], 0, 1).then_inc(S.ps, 1)
+        V.wait_ge(S.ps, 1)
+        v(V.tensor_scalar(T.pm[:, :], T.pi[:, :], 15, None, OP.bitwise_and))
+        vw()
+        v(V.tensor_scalar(T.k0[:, 0:1], T.pm[:, :], 16.0 * h, None, OP.add))
+    else:
+        v(V.memset(T.k0[:, :], (0.0, 256.0)[h - 2]))
     g.wait_ge(S.v, n[0])
-    g.remote_dma(T["s%d" % h][:, 0:1], T.k0[:, 0:1], S.th, S.loc, pid, rid, mask(en))
+    where = (T.s0[:, 0:1], T.s1[:, 0:1], T.z2[:, 0:2], T.crow[:, 256:257])[h]
+    send(r, (S.th, S.th, S.tz, S.tc)[h], T.k0[:, 0:2 if h == 2 else 1], where)
     if h == 0:
-        D.wait_ge(S.hs, 8)
+        D.wait_ge(S.hs, 16)
         for i in range(4):
             D.dma_start(T.wt[16 * i:16 * i + 16, :], T.hw[:, :]).then_inc(S.ld, 16)
         g.iota(T.nb[:, :], [[256, 8], [0, 2]], 0, 0, **SMALL).then_inc(S.ps, 1)
@@ -92,10 +101,10 @@ def relay(g, core, T, topo, r, h, ranks):
         v(V.tensor_copy(T.w2[:, 0:32:2], T.w16[:, :]))
         v(V.tensor_copy(T.w2[:, 1:32:2], T.w16[:, :]))
         V.wait_ge(S.ps, 4)
-        V.wait_ge(S.rl, 4)
+        V.wait_ge(S.rp, 4)
         for b in range(4):
             for a in range(4):
-                v(V.tensor_copy(T.ua[32 * a:32 * a + 32, 4 * b:4 * b + 4], T.rl[32 * b:32 * b + 32, :]))
+                v(V.tensor_copy(T.ua[32 * a:32 * a + 32, 4 * b:4 * b + 4], T.rp[32 * b:32 * b + 32, :]))
         vw()
         v(V.tensor_scalar(T.fu[:, :], T.ua[:, :], 256.0, None, OP.is_ge))
         v(V.tensor_tensor(T.u2[:, :], T.ua[:, :], T.nb[:, :], OP.add))
@@ -115,21 +124,23 @@ def relay(g, core, T, topo, r, h, ranks):
         v(V.tensor_copy(T.oy[:, :], T.pt[:, 0:512:32]))
 
     def place(f):
-        return 2 * [k for _, ks in roads(topo, cores, f) for k in ks].index(r)
+        return 2 * [k for _, k, _ in roads(topo, cores, f)].index(r)
     g.wait_ge(S.rl, 4)
-    g.remote_dma_fused([xfer(topo, core, cores[f], half[i], S.ab, T.rl[:, 2 * (f % 2):2 * (f % 2) + 2],
-                             T.lb[:, place(f):place(f) + 2]) for i, f in enumerate(ranks)], local_sem=S.loc)
+    send(f, S.ab, T.rl[:, 0:2], T.lb[:, place(f):place(f) + 2])
     if h == 0:
         g.wait_ge(S.v, n[0])
-        g.remote_dma(T.oy[:, 0:16], T.oy[:, 0:16], S.oy, S.loc, pid, rid, mask(en))
+        send(r, S.oy, T.oy[:, 0:16], T.oy[:, 0:16])
     here = slice(32 * plane.index(r), 32 * plane.index(r) + 32)
+    if near is not None:
+        g.wait_ge(S.ra, 4)
+        send(near, S.ac, u8(T.ra[:, :]), u8(T.ca[:, here]))
+        g.wait_ge(S.rz, 4)
+        send(near, S.ac, T.rz[:, :], T.da[:, here])
     g.wait_ge(S.rc, 4)
-    g.remote_dma_fused([xfer(topo, core, cores[f], half[i], S.ad, u8(T.rc[:, 32 * i:32 * i + 32]), u8(T.cb[:, here]))
-                        for i, f in enumerate(ranks)], local_sem=S.loc)
+    send(f, S.ad, u8(T.rc[:, :]), u8(T.cb[:, here]))
     g.wait_ge(S.rs, 4)
-    g.remote_dma_fused([xfer(topo, core, cores[f], half[i], S.ad, T.rs[:, 32 * i:32 * i + 32], T.db[:, here])
-                        for i, f in enumerate(ranks)], local_sem=S.loc)
-    g.wait_ge(S.loc, (5 - h) * len(en))
+    send(f, S.ad, T.rs[:, :], T.db[:, here])
+    g.wait_ge(S.loc, left[0])
 
 
 def rank_program(g, core, T, topo):
@@ -138,9 +149,9 @@ def rank_program(g, core, T, topo):
     if r is None:
         for k in range(len(cores)):
             if core in topo.cores_of(cores[k]):
-                for h, (c, ranks) in enumerate(roads(topo, cores, k)):
+                for h, (c, f, near) in enumerate(roads(topo, cores, k)):
                     if c == core:
-                        relay(g, core, T, topo, k, h, ranks)
+                        relay(g, core, T, topo, k, h, f, near)
         return
     S = T.sem
     plane = plane_of(topo, cores, r)
@@ -149,7 +160,8 @@ def rank_program(g, core, T, topo):
     me = plane.index(r)
     h_rid, h_pid = topo.addr(road[0][0], core)
     off = topo.engines(core, cores[others[0]])
-    on = [e for e in topo.engines(core, road[0][0]) if e not in off]
+    on = topo.engines(core, road[0][0])
+    on = [e for e in on if e not in off] + off
     V, A, D, P = g.vector, g.scalar, g.sync, g.tensor
     n = {"v": 0, "s": 0, "ps": 0}
 
@@ -178,46 +190,54 @@ def rank_program(g, core, T, topo):
     D.dma_start(T.xt[:, 0:1024], T.x[:, :]).then_inc(S.ldx, 16)
     D.dma_start(T.wb[:, :], T.w[:, :]).then_inc(S.ldw, 16)
 
-    g_p = ps(g.iota(T.pi[:, 0:1], [[0, 1]], 0, 1))
     g_v = ps(g.iota(T.vwin[:, 0:128], [[1, 128]], 128, 0, **SMALL))
+    g_k = ps(g.iota(T.cst[0:32, 0:128], [[-32, 4], [0, 32]], 256, -1, **SMALL))
+    g_p = ps(g.iota(T.pi[:, 0:1], [[0, 1]], 0, 1))
     g_c = ps(g.iota(T.cwin[:, 0:256], [[1, 256]], 0, 0, **SMALL))
-    for a in range(4):
-        g.wait_ge(S.ps, n["ps"])
-        g_k = ps(g.iota(T.cst[32 * a:32 * a + 32, 0:128], [[-32, 4], [0, 32]], 256 - 128 * (a // 2), -1, **SMALL))
     g.wait_ge(S.ld0, 16)
     g.remote_dma(T.hw[:, :], T.w0[:, 0:2], S.hs, S.loc, h_pid, h_rid, mask(on))
 
     v(V.memset(T.ones[:, :], 1.0))
-    v(V.memset(T.crow[:, 256:272], 256.0))
     v(V.memset(T.xt[:, 1024:4 * XW], 0.0))
-    v(V.memset(T.z2[:, :], 0.0))
+    V.wait_ge(S.ps, g_v)
+    for k, f in ((128, 2.0), (256, 4.0)):
+        v_v = v(V.tensor_scalar(T.vwin[:, k:2 * k], T.vwin[:, 0:k], f, None, OP.mult))
+        vw()
+    v(V.tensor_scalar(T.vwin[:, 512:1024], T.vwin[:, 0:512], 16.0, None, OP.mult))
+    v(V.tensor_scalar(T.vwin[:, 1024:1536], T.vwin[:, 0:512], 256.0, None, OP.mult))
+    A.wait_ge(S.v, v_v)
+    s_v = s(A.activation(T.vwin[:, 1536:2048], T.vwin[:, 0:512], COPY, scale=4096.0))
+    V.wait_ge(S.ps, g_k)
+    v_k = v(V.tensor_copy(T.cst[32:64, :], T.cst[0:32, :]))
     V.wait_ge(S.ps, g_p)
     v(V.tensor_scalar(T.odd[:, :], T.pi[:, :], 4, 1, OP.arith_shift_right, OP.bitwise_and))
+    V.wait_ge(S.v, v_k)
+    v(V.tensor_scalar(T.cst[64:128, :], T.cst[0:64, :], -128.0, None, OP.add))
+
+    V.wait_ge(S.ld, 64)
+    v(V.tensor_copy(T.w16[0:64, :], T.wt[:, :]))
+    v_w = v(V.tensor_copy(T.w16[64:128, :], T.wt[:, :]))
+    V.wait_ge(S.s, s_v)
     vw()
+    v_r = v(V.tensor_copy(T.row[:, 128:256], T.vwin[:, 0:2048].indirect(T.w16[:, 8:16])))
+    A.wait_ge(S.v, v_w)
+    A.wait_ge(S.s, s_v)
+    s_r = s(A.activation(T.row[:, 0:128], T.vwin[:, 0:2048].indirect(T.w16[:, 0:8]), COPY))
     for a in range(4):
         q = slice(32 * a, 32 * a + 32)
         v(V.tensor_scalar(T.gsc[q, :], T.odd[q, :], -0.75 * 16.0 ** -a, 16.0 ** -a, OP.mult, OP.add))
-    V.wait_ge(S.ps, g_v)
-    for k, f in ((128, 2.0), (256, 4.0), (512, 16.0), (1024, 256.0)):
-        v(V.tensor_scalar(T.vwin[:, k:2 * k], T.vwin[:, 0:k], f, None, OP.mult))
-        vw()
 
     A.wait_ge(S.ps, g_c)
     for k in (256, 512, 1024):
         k_s = s(A.activation(T.cwin[:, k:2 * k], T.cwin[:, 0:k], COPY))
         A.wait_ge(S.s, k_s)
-
-    V.wait_ge(S.ld, 64)
-    v(V.tensor_copy(T.w16[0:64, :], T.wt[:, :]))
-    v_w = v(V.tensor_copy(T.w16[64:128, :], T.wt[:, :]))
-    vw()
-    v(V.tensor_copy(T.row[:, :], T.vwin[:, 0:2048].indirect(T.w16[:, 0:16])))
-    A.wait_ge(S.v, v_w)
     s_cr = s(A.activation(T.crow[:, 0:256], T.cwin[:, 0:2048].indirect(T.w16[:, 0:16]), COPY))
     A.wait_ge(S.ldx, 16)
     for t in range(4):
         s_xs = s(A.activation(T.xs[:, XW * t:XW * t + XW], T.xt[:, t:4 * XW:4], COPY))
-    vw()
+
+    V.wait_ge(S.v, v_r)
+    V.wait_ge(S.s, s_r)
     halves = [slice(64 * h, 64 * h + 64) for h in range(2)]
     for h in range(2):
         v(V.transpose(T.rt[halves[h], 0:128], T.row[halves[h], 128 * h:128 * h + 128]))
@@ -225,61 +245,68 @@ def rank_program(g, core, T, topo):
     at = [0]
     for b in range(4):
         at.append(at[b] + 256 - 32 * b)
+    ne = [v(V.tensor_scalar(T.ne[:, at[b]:at[b + 1]], T.row[:, 32 * b:256], T.rt[:, 32 * b:32 * b + 1], None, OP.not_equal))
+          for b in range(4)]
+    sc = []
     for b in range(4):
-        v(V.tensor_scalar(T.ne[:, at[b]:at[b + 1]], T.row[:, 32 * b:256], T.rt[:, 32 * b:32 * b + 1], None, OP.not_equal))
-    vw()
+        V.wait_ge(S.v, ne[b])
+        sc.append(v(V.tensor_tensor_scan(T.sc[:, at[b]:at[b + 1]], T.ne[:, at[b]:at[b + 1]], T.ones[:, 0:256 - 32 * b],
+                                         0.0, OP.mult, OP.add)))
     for b in range(4):
-        v(V.tensor_tensor_scan(T.sc[:, at[b]:at[b + 1]], T.ne[:, at[b]:at[b + 1]], T.ones[:, 0:256 - 32 * b], 0.0, OP.mult, OP.add))
-    vw()
-    V.wait_ge(S.ps, g_k)
-    for b in range(4):
+        V.wait_ge(S.v, sc[b])
         v(V.tensor_scalar(T.fr[:, 32 * b:32 * b + 32], T.cst[:, 32 * b:32 * b + 32], T.sc[:, at[b + 1] - 1:at[b + 1]],
                           T.rt[:, 32 * b:32 * b + 1], OP.is_equal, OP.mult))
     vw()
+    qf = [v(V.transpose(T.qf[halves[h], 128 * h:128 * h + 128], T.fr[halves[h], 0:128])) for h in range(2)]
     for h in range(2):
-        v(V.transpose(T.qf[halves[h], 128 * h:128 * h + 128], T.fr[halves[h], 0:128]))
-    vw()
-    for h in range(2):
+        V.wait_ge(S.v, qf[h])
         v(V.tensor_copy(T.qf[halves[1 - h], 128 * h:128 * h + 128], T.qf[halves[h], 128 * h:128 * h + 128]))
     vw()
     v(V.tensor_scalar(T.ge[:, :], T.qf[:, :], T.gsc[:, 0:1], 128.0, OP.mult, OP.is_ge))
     v(V.tensor_scalar(T.gh[:, :], T.qf[:, :], T.gsc[:, 0:1], 512.0, OP.mult, OP.is_ge))
     vw()
     v(V.tensor_tensor_scan(T.cc[:, :], T.ge[:, :], T.gh[:, :], 0.0, OP.add, OP.subtract))
-    vw()
     V.wait_ge(S.th, 16)
-    for k in range(2):
-        v(V.tensor_scalar(T.le[:, 256 * k:256 * k + 256], T.cc[:, :], T["s%d" % k][:, 0:1], None, OP.is_le))
     vw()
+    le, nn = [], []
+    for k, t in enumerate((T.s0, T.s1)):
+        le.append(v(V.tensor_scalar(T.le[:, 256 * k:256 * k + 256], T.cc[:, :], t[:, 0:1], None, OP.is_le)))
     for k in range(2):
-        v(V.tensor_tensor_scan(T.nn[:, 256 * k:256 * k + 256], T.ones[:, :], T.le[:, 256 * k:256 * k + 256], 0.0, OP.mult, OP.add))
-    vw()
+        V.wait_ge(S.v, le[k])
+        nn.append(v(V.tensor_tensor_scan(T.nn[:, 256 * k:256 * k + 256], T.ones[:, :], T.le[:, 256 * k:256 * k + 256],
+                                         0.0, OP.mult, OP.add)))
+    V.wait_ge(S.tz, 8)
     for k in range(2):
+        V.wait_ge(S.v, nn[k])
         v(V.tensor_scalar(T.jj[:, 2 * k:2 * k + 2], T.z2[:, :], T.nn[:, 256 * k + 255:256 * k + 256], None, OP.add))
-    vw()
+    V.wait_ge(S.tc, 8)
     V.wait_ge(S.s, s_cr)
-    v(V.tensor_copy(T.lg[:, :], T.crow[:, 0:272].indirect(T.jj[:, 0:4])))
+    vw()
+    v(V.tensor_copy(T.lg[:, :], T.crow[:, 0:257].indirect(T.jj[:, 0:4])))
     vw()
     v(V.transpose(T.lt[:, :], T.lg[:, :]))
     vw()
     for k in range(2):
         v_msg = v(V.tensor_copy(T.msg[:, 2 * k:2 * k + 2], T.lt[:, 16 * k:64:32]))
-    vw()
 
-    g.wait_ge(S.v, v_msg)
-    g.remote_dma_fused([xfer(topo, core, c, on[4 * i:4 * i + 4], S.rl, T.msg[:, 0:4], T.rl[:, 0:4])
-                        for i, (c, _) in enumerate(road)], local_sem=S.loc)
+    def of(f):
+        return T.msg[:, 2 * (f % 2):2 * (f % 2) + 2]
 
     def among(f):
         return 2 * [k for k in plane if k != f].index(r)
-    g.remote_dma_fused([xfer(topo, core, cores[f], off[2 * i:2 * i + 2], S.aa, T.msg[:, 2 * (f % 2):2 * (f % 2) + 2],
-                             T.la[:, among(f):among(f) + 2]) for i, f in enumerate(others)], local_sem=S.loc)
+    g.wait_ge(S.v, v_msg)
+    g.remote_dma_fused([xfer(topo, core, c, on[4 * i:4 * i + 4], S.rl, of(f), T.rl[:, 0:2])
+                        for i, (c, f, _) in enumerate(road)], local_sem=S.loc)
+    g.remote_dma_fused([xfer(topo, core, cores[f], off[2 * i:2 * i + 2], S.aa, of(f), T.la[:, among(f):among(f) + 2])
+                        for i, f in enumerate(others)], local_sem=S.loc)
+    g.remote_dma(T.rp[:, 0:4], T.msg[:, 0:4], S.rp, S.loc, h_pid, h_rid, mask(on[0:4]))
 
-    mq = slice(32 * (r // 2), 32 * (r // 2) + 32)
-    for a in range(4):
-        v(V.tensor_copy(T.oa[32 * a:32 * a + 32, 0:2], T.msg[mq, 2 * (r % 2):2 * (r % 2) + 2]))
     V.wait_ge(S.ldw, 16)
     v_qw = v(V.quantize_mx(T.qw[:, :], T.pw[:, :], T.wb[:, :]))
+    mq = slice(32 * (r // 2), 32 * (r // 2) + 32)
+    V.wait_ge(S.v, v_msg)
+    for a in range(4):
+        v(V.tensor_copy(T.oa[32 * a:32 * a + 32, 0:2], T.msg[mq, 2 * (r % 2):2 * (r % 2) + 2]))
 
     def serve(lists, offs, o0, tile, codes, plane8, sem, arrivals):
         V.wait_ge(sem, arrivals)
@@ -298,29 +325,29 @@ def rank_program(g, core, T, topo):
     V.wait_ge(S.s, s_xs)
     A.wait_ge(S.s, s_xs)
     v_qa = serve(T.la, T.oa, 2, T.ta, T.qa, T.pa, S.aa, 6)
-    v_qb = serve(T.lb, T.ob, 0, T.tb, T.qb, T.pb, S.ab, 16)
+    v_qb = serve(T.lb, T.ob, 0, T.tb, T.qb, T.pb, S.ab, 32)
 
+    def codes(q, i):
+        return u8(q[:, 32 * i:32 * i + 32])
+
+    def scales(p, i):
+        return p[:, 32 * i:32 * i + 32]
+    for done, first, view, src, dst, sem in ((v_qa, 1, codes, T.qa, T.ra, S.ra), (v_qa, 1, scales, T.pa, T.rz, S.rz),
+                                             (v_qb, 0, codes, T.qb, T.rc, S.rc), (v_qb, 0, scales, T.pb, T.rs, S.rs)):
+        g.wait_ge(S.v, done)
+        g.remote_dma_fused([xfer(topo, core, road[h][0], on[4 * h:4 * h + 4], sem, view(src, h), view(dst, 0))
+                            for h in range(first, 4)], local_sem=S.loc)
+    g.wait_ge(S.loc, 16 + 16 + 6 + 4 + 2 * 12 + 2 * 16)
     here = slice(32 * me, 32 * me + 32)
-    g.wait_ge(S.v, v_qa)
-    g.remote_dma_fused([xfer(topo, core, cores[f], off[2 * i:2 * i + 2], S.ac, u8(T.qa[:, 32 + 32 * i:64 + 32 * i]),
-                             u8(T.ca[:, here])) for i, f in enumerate(others)], local_sem=S.loc)
-    g.remote_dma_fused([xfer(topo, core, cores[f], off[2 * i:2 * i + 2], S.ac, T.pa[:, 32 + 32 * i:64 + 32 * i],
-                             T.da[:, here]) for i, f in enumerate(others)], local_sem=S.loc)
-    g.wait_ge(S.v, v_qb)
-    g.remote_dma_fused([xfer(topo, core, c, on[4 * i:4 * i + 4], S.rc, u8(T.qb[:, 64 * i:64 * i + 64]), u8(T.rc[:, :]))
-                        for i, (c, _) in enumerate(road)], local_sem=S.loc)
-    g.remote_dma_fused([xfer(topo, core, c, on[4 * i:4 * i + 4], S.rs, T.pb[:, 64 * i:64 * i + 64], T.rs[:, :])
-                        for i, (c, _) in enumerate(road)], local_sem=S.loc)
-    g.wait_ge(S.loc, 8 + 3 * 8 + 3 * 6)
     D.wait_ge(S.v, v_qa)
     D.dma_start(u8(T.ca[:, here]), u8(T.qa[:, 0:32])).then_inc(S.own, 16)
     D.dma_start(T.da[:, here], T.pa[:, 0:32]).then_inc(S.own, 16)
 
     P.wait_ge(S.v, v_qw)
-    P.wait_ge(S.ac, 12)
+    P.wait_ge(S.ac, 48)
     P.wait_ge(S.own, 32)
     P.matmul_mx(T.m0[:, 0:128], T.qw[:, :], T.pw[:, :], T.ca[:, :], T.da[:, :], True, True).then_inc(S.te, 1)
-    P.wait_ge(S.ad, 32)
+    P.wait_ge(S.ad, 64)
     P.matmul_mx(T.m1[:, 0:128], T.qw[:, :], T.pw[:, :], T.cb[:, :], T.db[:, :], True, True).then_inc(S.te, 1)
     A.wait_ge(S.te, 1)
     s_y = s(A.activation(T.ys[:, 0:128], T.m0[:, 0:128], COPY))

from concourse.bass import DstId, RemoteDMATransfer
from concourse.mybir import dt, AluOpType, ActivationFunctionType

OP = AluOpType
COPY = ActivationFunctionType.Copy
XW = 272
PW = 2432
SMALL = {"allow_small_or_imprecise_dtypes": True}

SCRATCH = {"wt": ("sbuf", [64, 16], "int32"), "hw": ("dram", [128, 2], "int32"),
           "m0": ("psum", [128, 512], "float32"), "m1": ("psum", [128, 512], "float32")}
for _t, _b in (("int32", "pi 1 pm 1 odd 1 w0 2"),
               ("uint16", "w16 16 w2 32 jj 4 msg 4 la 6 lb 8 oa 8 ob 8 rl 2 rp 4 ou 16 oy 16"),
               ("float32", "gsc 1 ua 16 fu 16 u1 16 u2 16 u3 16 nb 16 dd 16 ys 256 yo 256"),
               ("bfloat16", "k0 2 z2 2 s0 1 s1 1 vwin 2048 pos %d cwin 2048 ones 256 cst 128 row 256 crow 272 rt 128 "
                            "ne 832 sc 832 fr 128 qf 256 ge 256 gh 256 cc 256 le 512 nn 512 lg 64 lt 64 xt %d xs %d "
                            "wb 512 ta 512 tb 512 vp 256 pr 512 pt 512" % (PW, 4 * XW, 4 * XW)),
               ("float8_e4m3fn_x4", "qw 128 qa 128 qb 128 ca 128 cb 128 rc 32 ra 32"),
               ("uint8", "pw 128 pa 128 pb 128 da 128 db 128 rs 32 rz 32")):
    _w = _b.split()
    for _i in range(0, len(_w), 2):
        SCRATCH[_w[_i]] = ("sbuf", [128, int(_w[_i + 1])], _t)
SEMAPHORES = "ld ldx ldw ld0 v s ps te aa ab ac ad own st su loc rl rp rc rs ra rz th tz tc hs oy".split()


def plane_of(topo, cores, r):
    return [k for k in range(len(cores)) if k == r or topo.same_plane(cores[k], cores[r])]


def roads(topo, cores, r):
    mine = plane_of(topo, cores, r)
    far = [k for k in range(len(cores)) if k not in mine]
    near = [None] + [k for k in mine if k != r]
    c = cores[r]
    able = [k for k in topo.cores_of(c) if k != c and all(topo.may_write(k, cores[f]) for f in far)]
    able = [k for k in able if topo.die(k) == topo.die(c)] + [k for k in able if topo.die(k) != topo.die(c)]
    a = mine.index(r)
    return [(able[h], far[(h - a) % len(far)], near[h]) for h in range(len(far))]


def mask(engines):
    return sum(1 << k for k in engines)


def xfer(topo, src_core, dst_core, engines, sem, src, dst):
    rid, pid = topo.addr(dst_core, src_core)
    return RemoteDMATransfer(dst_ids=[DstId(rid=rid, pnc=pid)], dma_engine_mask=mask(engines),
                             remote_sem=sem, srcs=[src], dsts=[dst], alu_op=0)


def u8(view):
    return view.bitcast(dt.uint8)


def relay(g, core, T, topo, r, h, f, near):
    cores = T.cores
    en = topo.engines(core, cores[f])
    plane = plane_of(topo, cores, r)
    far = [k for k in range(len(cores)) if k not in plane]
    V, D, S = g.vector, g.sync, T.sem
    n = [0]
    left = [0]

    def v(call):
        call.then_inc(S.v, 1)
        n[0] += 1

    def vw():
        V.wait_ge(S.v, n[0])

    def send(k, sem, src, dst):
        rid, pid = topo.addr(cores[k], core)
        g.remote_dma(dst, src, sem, S.loc, pid, rid, mask(en))
        left[0] += len(en)
    if h < 2:
        g.iota(T.pi[:, 0:1], [[0, 1]], 0, 1).then_inc(S.ps, 1)
        V.wait_ge(S.ps, 1)
        v(V.tensor_scalar(T.pm[:, :], T.pi[:, :], 15, None, OP.bitwise_and))
        vw()
        v(V.tensor_scalar(T.k0[:, 0:1], T.pm[:, :], 16.0 * h, None, OP.add))
    else:
        v(V.memset(T.k0[:, :], (0.0, 256.0)[h - 2]))
    g.wait_ge(S.v, n[0])
    where = (T.s0[:, 0:1], T.s1[:, 0:1], T.z2[:, 0:2], T.crow[:, 256:257])[h]
    send(r, (S.th, S.th, S.tz, S.tc)[h], T.k0[:, 0:2 if h == 2 else 1], where)
    if h == 0:
        D.wait_ge(S.hs, 16)
        for i in range(4):
            D.dma_start(T.wt[16 * i:16 * i + 16, :], T.hw[:, :]).then_inc(S.ld, 16)
        g.iota(T.nb[:, :], [[256, 8], [0, 2]], 0, 0, **SMALL).then_inc(S.ps, 1)
        g.iota(T.dd[:, :], [[-224, 8], [16, 2]], 1792, 1, **SMALL).then_inc(S.ps, 1)
        col = [32 * (plane.index(k) if k in plane else 4 + far.index(k)) for k in range(8)]
        step = col[1] - col[0]
        assert col == [col[0] + 32 * (k // 2) + step * (k % 2) for k in range(8)]
        g.iota(T.vp[:, :], [[32, 4], [step, 2], [1, 32]], col[0], 0, **SMALL).then_inc(S.ps, 1)
        v(V.memset(T.pos[:, 0:2048], 0.0))
        V.wait_ge(S.ld, 64)
        v(V.tensor_copy(T.w16[0:64, :], T.wt[:, :]))
        v(V.tensor_copy(T.w16[64:128, :], T.wt[:, :]))
        vw()
        v(V.tensor_copy(T.w2[:, 0:32:2], T.w16[:, :]))
        v(V.tensor_copy(T.w2[:, 1:32:2], T.w16[:, :]))
        V.wait_ge(S.ps, 4)
        V.wait_ge(S.rp, 4)
        for b in range(4):
            for a in range(4):
                v(V.tensor_copy(T.ua[32 * a:32 * a + 32, 4 * b:4 * b + 4], T.rp[32 * b:32 * b + 32, :]))
        vw()
        v(V.tensor_scalar(T.fu[:, :], T.ua[:, :], 256.0, None, OP.is_ge))
        v(V.tensor_tensor(T.u2[:, :], T.ua[:, :], T.nb[:, :], OP.add))
        vw()
        v(V.tensor_tensor(T.u1[:, :], T.fu[:, :], T.dd[:, :], OP.mult))
        vw()
        v(V.tensor_tensor(T.u3[:, :], T.u1[:, :], T.u2[:, :], OP.add))
        vw()
        v(V.tensor_copy(T.ou[:, :], T.u3[:, :]))
        vw()
        v(V.tensor_copy(T.pos[:, 0:PW].indirect(T.ou[:, 0:16]), T.vp[:, :]))
        vw()
        v(V.tensor_copy(T.pr[:, :], T.pos[:, 0:2048].indirect(T.w2[:, 0:32])))
        vw()
        v(V.transpose(T.pt[:, :], T.pr[:, :]))
        vw()
        v(V.tensor_copy(T.oy[:, :], T.pt[:, 0:512:32]))

    def place(f):
        return 2 * [k for _, k, _ in roads(topo, cores, f)].index(r)
    g.wait_ge(S.rl, 4)
    send(f, S.ab, T.rl[:, 0:2], T.lb[:, place(f):place(f) + 2])
    if h == 0:
        g.wait_ge(S.v, n[0])
        send(r, S.oy, T.oy[:, 0:16], T.oy[:, 0:16])
    here = slice(32 * plane.index(r), 32 * plane.index(r) + 32)
    if near is not None:
        g.wait_ge(S.ra, 4)
        send(near, S.ac, u8(T.ra[:, :]), u8(T.ca[:, here]))
        g.wait_ge(S.rz, 4)
        send(near, S.ac, T.rz[:, :], T.da[:, here])
    g.wait_ge(S.rc, 4)
    send(f, S.ad, u8(T.rc[:, :]), u8(T.cb[:, here]))
    g.wait_ge(S.rs, 4)
    send(f, S.ad, T.rs[:, :], T.db[:, here])
    g.wait_ge(S.loc, left[0])


def rank_program(g, core, T, topo):
    cores = T.cores
    r = T.rank_of(core)
    if r is None:
        for k in range(len(cores)):
            if core in topo.cores_of(cores[k]):
                for h, (c, f, near) in enumerate(roads(topo, cores, k)):
                    if c == core:
                        relay(g, core, T, topo, k, h, f, near)
        return
    S = T.sem
    plane = plane_of(topo, cores, r)
    others = [k for k in plane if k != r]
    road = roads(topo, cores, r)
    me = plane.index(r)
    h_rid, h_pid = topo.addr(road[0][0], core)
    off = topo.engines(core, cores[others[0]])
    on = topo.engines(core, road[0][0])
    on = [e for e in on if e not in off] + off
    V, A, D, P = g.vector, g.scalar, g.sync, g.tensor
    n = {"v": 0, "s": 0, "ps": 0}

    def count(name, call):
        call.then_inc(S[name], 1)
        n[name] += 1
        return n[name]

    def v(call):
        return count("v", call)

    def s(call):
        return count("s", call)

    def ps(call):
        return count("ps", call)

    def vw():
        V.wait_ge(S.v, n["v"])

    D.dma_start(T.wt[0:16, :], T.want[:, :]).then_inc(S.ld, 16)
    A.dma_start(T.wt[16:32, :], T.want[:, :]).then_inc(S.ld, 16)
    D.dma_start(T.wt[32:48, :], T.want[:, :]).then_inc(S.ld, 16)
    A.dma_start(T.wt[48:64, :], T.want[:, :]).then_inc(S.ld, 16)
    A.dma_start(T.w0[:, :], T.want[:, :]).then_inc(S.ld0, 16)
    D.dma_start(T.xt[:, 0:1024], T.x[:, :]).then_inc(S.ldx, 16)
    D.dma_start(T.wb[:, :], T.w[:, :]).then_inc(S.ldw, 16)

    g_v = ps(g.iota(T.vwin[:, 0:128], [[1, 128]], 128, 0, **SMALL))
    g_k = ps(g.iota(T.cst[0:32, 0:128], [[-32, 4], [0, 32]], 256, -1, **SMALL))
    g_p = ps(g.iota(T.pi[:, 0:1], [[0, 1]], 0, 1))
    g_c = ps(g.iota(T.cwin[:, 0:256], [[1, 256]], 0, 0, **SMALL))
    g.wait_ge(S.ld0, 16)
    g.remote_dma(T.hw[:, :], T.w0[:, 0:2], S.hs, S.loc, h_pid, h_rid, mask(on))

    v(V.memset(T.ones[:, :], 1.0))
    v(V.memset(T.xt[:, 1024:4 * XW], 0.0))
    V.wait_ge(S.ps, g_v)
    for k, f in ((128, 2.0), (256, 4.0)):
        v_v = v(V.tensor_scalar(T.vwin[:, k:2 * k], T.vwin[:, 0:k], f, None, OP.mult))
        vw()
    v(V.tensor_scalar(T.vwin[:, 512:1024], T.vwin[:, 0:512], 16.0, None, OP.mult))
    v(V.tensor_scalar(T.vwin[:, 1024:1536], T.vwin[:, 0:512], 256.0, None, OP.mult))
    A.wait_ge(S.v, v_v)
    s_v = s(A.activation(T.vwin[:, 1536:2048], T.vwin[:, 0:512], COPY, scale=4096.0))
    V.wait_ge(S.ps, g_k)
    v_k = v(V.tensor_copy(T.cst[32:64, :], T.cst[0:32, :]))
    V.wait_ge(S.ps, g_p)
    v(V.tensor_scalar(T.odd[:, :], T.pi[:, :], 4, 1, OP.arith_shift_right, OP.bitwise_and))
    V.wait_ge(S.v, v_k)
    v(V.tensor_scalar(T.cst[64:128, :], T.cst[0:64, :], -128.0, None, OP.add))

    V.wait_ge(S.ld, 64)
    v(V.tensor_copy(T.w16[0:64, :], T.wt[:, :]))
    v_w = v(V.tensor_copy(T.w16[64:128, :], T.wt[:, :]))
    V.wait_ge(S.s, s_v)
    vw()
    v_r = v(V.tensor_copy(T.row[:, 128:256], T.vwin[:, 0:2048].indirect(T.w16[:, 8:16])))
    A.wait_ge(S.v, v_w)
    A.wait_ge(S.s, s_v)
    s_r = s(A.activation(T.row[:, 0:128], T.vwin[:, 0:2048].indirect(T.w16[:, 0:8]), COPY))
    for a in range(4):
        q = slice(32 * a, 32 * a + 32)
        v(V.tensor_scalar(T.gsc[q, :], T.odd[q, :], -0.75 * 16.0 ** -a, 16.0 ** -a, OP.mult, OP.add))

    A.wait_ge(S.ps, g_c)
    for k in (256, 512, 1024):
        k_s = s(A.activation(T.cwin[:, k:2 * k], T.cwin[:, 0:k], COPY))
        A.wait_ge(S.s, k_s)
    s_cr = s(A.activation(T.crow[:, 0:256], T.cwin[:, 0:2048].indirect(T.w16[:, 0:16]), COPY))
    A.wait_ge(S.ldx, 16)
    for t in range(4):
        s_xs = s(A.activation(T.xs[:, XW * t:XW * t + XW], T.xt[:, t:4 * XW:4], COPY))

    V.wait_ge(S.v, v_r)
    V.wait_ge(S.s, s_r)
    halves = [slice(64 * h, 64 * h + 64) for h in range(2)]
    for h in range(2):
        v(V.transpose(T.rt[halves[h], 0:128], T.row[halves[h], 128 * h:128 * h + 128]))
    vw()
    at = [0]
    for b in range(4):
        at.append(at[b] + 256 - 32 * b)
    ne = [v(V.tensor_scalar(T.ne[:, at[b]:at[b + 1]], T.row[:, 32 * b:256], T.rt[:, 32 * b:32 * b + 1], None, OP.not_equal))
          for b in range(4)]
    sc = []
    for b in range(4):
        V.wait_ge(S.v, ne[b])
        sc.append(v(V.tensor_tensor_scan(T.sc[:, at[b]:at[b + 1]], T.ne[:, at[b]:at[b + 1]], T.ones[:, 0:256 - 32 * b],
                                         0.0, OP.mult, OP.add)))
    for b in range(4):
        V.wait_ge(S.v, sc[b])
        v(V.tensor_scalar(T.fr[:, 32 * b:32 * b + 32], T.cst[:, 32 * b:32 * b + 32], T.sc[:, at[b + 1] - 1:at[b + 1]],
                          T.rt[:, 32 * b:32 * b + 1], OP.is_equal, OP.mult))
    vw()
    qf = [v(V.transpose(T.qf[halves[h], 128 * h:128 * h + 128], T.fr[halves[h], 0:128])) for h in range(2)]
    for h in range(2):
        V.wait_ge(S.v, qf[h])
        v(V.tensor_copy(T.qf[halves[1 - h], 128 * h:128 * h + 128], T.qf[halves[h], 128 * h:128 * h + 128]))
    vw()
    v(V.tensor_scalar(T.ge[:, :], T.qf[:, :], T.gsc[:, 0:1], 128.0, OP.mult, OP.is_ge))
    v(V.tensor_scalar(T.gh[:, :], T.qf[:, :], T.gsc[:, 0:1], 512.0, OP.mult, OP.is_ge))
    vw()
    v(V.tensor_tensor_scan(T.cc[:, :], T.ge[:, :], T.gh[:, :], 0.0, OP.add, OP.subtract))
    V.wait_ge(S.th, 16)
    vw()
    le, nn = [], []
    for k, t in enumerate((T.s0, T.s1)):
        le.append(v(V.tensor_scalar(T.le[:, 256 * k:256 * k + 256], T.cc[:, :], t[:, 0:1], None, OP.is_le)))
    for k in range(2):
        V.wait_ge(S.v, le[k])
        nn.append(v(V.tensor_tensor_scan(T.nn[:, 256 * k:256 * k + 256], T.ones[:, :], T.le[:, 256 * k:256 * k + 256],
                                         0.0, OP.mult, OP.add)))
    V.wait_ge(S.tz, 8)
    for k in range(2):
        V.wait_ge(S.v, nn[k])
        v(V.tensor_scalar(T.jj[:, 2 * k:2 * k + 2], T.z2[:, :], T.nn[:, 256 * k + 255:256 * k + 256], None, OP.add))
    V.wait_ge(S.tc, 8)
    V.wait_ge(S.s, s_cr)
    vw()
    v(V.tensor_copy(T.lg[:, :], T.crow[:, 0:257].indirect(T.jj[:, 0:4])))
    vw()
    v(V.transpose(T.lt[:, :], T.lg[:, :]))
    vw()
    for k in range(2):
        v_msg = v(V.tensor_copy(T.msg[:, 2 * k:2 * k + 2], T.lt[:, 16 * k:64:32]))

    def of(f):
        return T.msg[:, 2 * (f % 2):2 * (f % 2) + 2]

    def among(f):
        return 2 * [k for k in plane if k != f].index(r)
    g.wait_ge(S.v, v_msg)
    g.remote_dma_fused([xfer(topo, core, c, on[4 * i:4 * i + 4], S.rl, of(f), T.rl[:, 0:2])
                        for i, (c, f, _) in enumerate(road)], local_sem=S.loc)
    g.remote_dma_fused([xfer(topo, core, cores[f], off[2 * i:2 * i + 2], S.aa, of(f), T.la[:, among(f):among(f) + 2])
                        for i, f in enumerate(others)], local_sem=S.loc)
    g.remote_dma(T.rp[:, 0:4], T.msg[:, 0:4], S.rp, S.loc, h_pid, h_rid, mask(on[0:4]))

    V.wait_ge(S.ldw, 16)
    v_qw = v(V.quantize_mx(T.qw[:, :], T.pw[:, :], T.wb[:, :]))
    mq = slice(32 * (r // 2), 32 * (r // 2) + 32)
    V.wait_ge(S.v, v_msg)
    for a in range(4):
        v(V.tensor_copy(T.oa[32 * a:32 * a + 32, 0:2], T.msg[mq, 2 * (r % 2):2 * (r % 2) + 2]))

    def serve(lists, offs, o0, tile, codes, plane8, sem, arrivals):
        V.wait_ge(sem, arrivals)
        for a in range(4):
            v_o = v(V.tensor_copy(offs[32 * a:32 * a + 32, o0:8], lists[mq, :]))
        vw()
        for t in range(2):
            v(V.tensor_copy(tile[:, t:512:4], T.xs[:, XW * t:XW * t + XW].indirect(offs[:, 0:8])))
        A.wait_ge(S.v, v_o)
        for t in range(2, 4):
            s_t = s(A.activation(tile[:, t:512:4], T.xs[:, XW * t:XW * t + XW].indirect(offs[:, 0:8]), COPY))
        vw()
        V.wait_ge(S.s, s_t)
        return v(V.quantize_mx(codes[:, :], plane8[:, :], tile[:, :]))

    V.wait_ge(S.s, s_xs)
    A.wait_ge(S.s, s_xs)
    v_qa = serve(T.la, T.oa, 2, T.ta, T.qa, T.pa, S.aa, 6)
    v_qb = serve(T.lb, T.ob, 0, T.tb, T.qb, T.pb, S.ab, 32)

    def codes(q, i):
        return u8(q[:, 32 * i:32 * i + 32])

    def scales(p, i):
        return p[:, 32 * i:32 * i + 32]
    for done, first, view, src, dst, sem in ((v_qa, 1, codes, T.qa, T.ra, S.ra), (v_qa, 1, scales, T.pa, T.rz, S.rz),
                                             (v_qb, 0, codes, T.qb, T.rc, S.rc), (v_qb, 0, scales, T.pb, T.rs, S.rs)):
        g.wait_ge(S.v, done)
        g.remote_dma_fused([xfer(topo, core, road[h][0], on[4 * h:4 * h + 4], sem, view(src, h), view(dst, 0))
                            for h in range(first, 4)], local_sem=S.loc)
    g.wait_ge(S.loc, 16 + 16 + 6 + 4 + 2 * 12 + 2 * 16)
    here = slice(32 * me, 32 * me + 32)
    D.wait_ge(S.v, v_qa)
    D.dma_start(u8(T.ca[:, here]), u8(T.qa[:, 0:32])).then_inc(S.own, 16)
    D.dma_start(T.da[:, here], T.pa[:, 0:32]).then_inc(S.own, 16)

    P.wait_ge(S.v, v_qw)
    P.wait_ge(S.ac, 48)
    P.wait_ge(S.own, 32)
    P.matmul_mx(T.m0[:, 0:128], T.qw[:, :], T.pw[:, :], T.ca[:, :], T.da[:, :], True, True).then_inc(S.te, 1)
    P.wait_ge(S.ad, 64)
    P.matmul_mx(T.m1[:, 0:128], T.qw[:, :], T.pw[:, :], T.cb[:, :], T.db[:, :], True, True).then_inc(S.te, 1)
    A.wait_ge(S.te, 1)
    s_y = s(A.activation(T.ys[:, 0:128], T.m0[:, 0:128], COPY))
    V.wait_ge(S.oy, 8)
    A.wait_ge(S.oy, 8)
    V.wait_ge(S.te, 2)
    v_y = v(V.tensor_copy(T.ys[:, 128:256], T.m1[:, 0:128]))
    vw()
    V.wait_ge(S.s, s_y)
    v_o = v(V.tensor_copy(T.yo[:, 0:128], T.ys[:, 0:256].indirect(T.oy[:, 0:8])))
    A.wait_ge(S.v, v_y)
    A.wait_ge(S.s, s_y)
    s_o = s(A.activation(T.yo[:, 128:256], T.ys[:, 0:256].indirect(T.oy[:, 8:16]), COPY))
    D.wait_ge(S.v, v_o)
    D.dma_start(T.y[:, 0:128], T.yo[:, 0:128]).then_inc(S.st, 16)
    A.wait_ge(S.s, s_o)
    A.dma_start(T.y[:, 128:256], T.yo[:, 128:256]).then_inc(S.su, 16)
    D.wait_ge(S.st, 16)
    A.wait_ge(S.su, 16)
